import numpy as np
import ml_dtypes


def mxq(x, axis, fmt="e4m3"):
    dtype, down = {"e4m3": (ml_dtypes.float8_e4m3fn, 7), "e5m2": (ml_dtypes.float8_e5m2, 14)}[fmt]
    v = np.moveaxis(np.asarray(x, np.float32).astype(ml_dtypes.bfloat16).astype(np.float64), axis, -1)
    blocks = v.reshape(v.shape[:-1] + (-1, 32))
    amax = np.abs(blocks).max(-1, keepdims=True)
    byte = np.maximum(np.where(amax > 0, np.frexp(amax)[1] - 1 + 127, 0) - down, 1)
    scale = np.exp2(byte - 127.0)
    codes = (blocks / scale).astype(np.float32).astype(dtype).astype(np.float64)
    return np.moveaxis((codes * scale).reshape(v.shape), -1, axis)


WIDE = False


def mx_kscale(k):
    if not WIDE:
        return np.ones(k)
    levels = np.array([10, -10, 5, -5, 0])
    if k % 512:
        return np.exp2(np.random.permutation(np.resize(levels, k // 32))).repeat(32)
    a = np.empty((k // 512, 16))
    for p in range(k // 512):
        a[p, :8] = np.random.permutation(np.resize(levels, 8))
        for g in range(8):
            far = levels[np.abs(levels - a[p, g]) >= 10]
            a[p, g + 8] = far[np.random.randint(len(far))]
    return np.exp2(a.ravel()).repeat(32)


def f64(x):
    return np.asarray(x).astype(np.float64)


def striped(idx):
    return np.tile(idx.reshape(-1, 16).T, (8, 1)).astype(np.uint16)


def unstriped(offs):
    return offs[:16].T.reshape(-1).astype(np.int64)


def striped8(idx):
    return np.concatenate([x.reshape(-1, 16).T for x in idx]).astype(np.uint16)


def runs(offs, k):
    lists = np.stack([offs[16 * r : 16 * r + 16].T.reshape(-1) for r in range(8)]).astype(np.int64)
    return lists[np.arange(k) % 512 // 64]


def pack_weight(w):
    k, n = w.shape
    w = f64(np.asarray(w, np.float32).astype(ml_dtypes.bfloat16)).reshape(k // 32, 32, n)
    amax = np.abs(w).max(1)
    byte = np.clip(np.where(amax > 0, np.frexp(amax)[1] - 1 + 127 - 7, 1), 1, 254)
    scaled = (w * np.exp2(127.0 - byte)[:, None, :]).reshape(k, n).astype(np.float32)
    words = np.ascontiguousarray(scaled.reshape(k // 512, 128, 4, n).transpose(0, 1, 3, 2)).astype(ml_dtypes.float8_e4m3fn).view(np.uint8)
    return words, np.ascontiguousarray(byte.astype(np.uint8).reshape(k // 512, 16, n))


def unpack_weight(words, scales):
    g, p, n, _ = words.shape
    vals = np.ascontiguousarray(words).view(ml_dtypes.float8_e4m3fn).astype(np.float64) * np.repeat(np.exp2(scales.astype(np.float64) - 127.0), 8, axis=1)[..., None]
    return vals.transpose(0, 1, 3, 2).reshape(g * 512, n)

def planes(y):
    n, m = y.shape
    v = y.astype(np.float32).astype(ml_dtypes.bfloat16).astype(np.float64).reshape(n // 32, 32, m)
    top = np.abs(v).max(1)
    byte = np.clip(np.where(top > 0, np.frexp(top)[1] - 1 + 127 - 7, 1), 1, 254)
    codes = (v * np.exp2(127.0 - byte)[:, None, :]).reshape(n, m).astype(np.float32).astype(ml_dtypes.float8_e4m3fn).view(np.uint8)
    words = codes.reshape(n // 512, 128, 4, m).transpose(0, 1, 3, 2)
    return np.ascontiguousarray(words), np.ascontiguousarray(byte.astype(np.uint8).reshape(n // 512, 16, m))


K, T, S, G, H, W = 512, 2048, 512, 2048, 512, 256


def setup_inputs():
    n = np.random.standard_normal
    s = mx_kscale(K)[:, None]
    packed_xT = pack_weight(n((K, T)) * s)
    packed_dT = pack_weight(n((K, G)) / s)
    perm = np.stack([np.random.permutation(S) for _ in range(8)])
    return {
        "x_words": packed_xT[0],
        "x_scales": packed_xT[1],
        "d_words": packed_dT[0],
        "d_scales": packed_dT[1],
        "gs": (np.random.uniform(0.5, 1.5, (K, 1)) * s).astype(np.float32),
        "offs": striped(np.random.permutation(T)[:S]),
        "ci": striped(np.random.permutation(G)[:H]),
        "k1": striped8(np.random.randint(0, G, (8, H))),
        "n1": striped8(perm[:, :W]),
        "n2": striped8(perm[:, W:]),
        "n3": striped8(np.stack([np.random.permutation(S) for _ in range(8)])),
    }


def reference(x_words, x_scales, d_words, d_scales, gs, offs, ci, k1, n1, n2, n3):
    d_k1 = unpack_weight(d_words, d_scales)[np.arange(K)[:, None], runs(k1, K)]
    d_ci = unpack_weight(d_words, d_scales)[:, unstriped(ci)]
    xq = unpack_weight(x_words, x_scales)[:, unstriped(offs)]
    s = 0.0625 * (d_ci.T @ xq)
    z = f64(gs) * s
    h = 0.0625 * ((d_k1.T @ mxq(z, 0, "e4m3")))
    pa = h[np.arange(H)[:, None], runs(n1, H)]
    pb = h[np.arange(H)[:, None], runs(n2, H)]
    rb = np.minimum(pa, pb)
    ra = np.maximum(pa, pb)
    ds = np.zeros((H, S))
    ds[np.arange(H)[:, None], runs(n1, H)] = ra
    dt = ds.copy()
    dt[np.arange(H)[:, None], runs(n2, H)] = rb
    out_0 = dt - (dt[np.arange(H)[:, None], runs(n3, H)])
    return (out_0,) + planes(out_0)

@@ -1,0 +1,243 @@
+from contextlib import ExitStack
+
+import concourse.mybir as mybir
+
+F32 = mybir.dt.float32
+BF16 = mybir.dt.bfloat16
+I32 = mybir.dt.int32
+U32 = mybir.dt.uint32
+U16 = mybir.dt.uint16
+U8 = mybir.dt.uint8
+FP8X4 = mybir.dt.float8_e4m3fn_x4
+ALU = mybir.AluOpType
+COPY = mybir.ActivationFunctionType.Copy
+
+P = 128
+PACK = 4
+TABLE = 2048
+S = 512
+HALF = S // 2
+QUARTER = S // 4
+
+FLOPS = 2 * 2 * 512 * 512 * 512
+
+
+def tile_picked_dwqiordd_none_po_kernel(
+    tc, x_words, x_scales, d_words, d_scales, gs, offs, ci, k1, n1, n2, n3, out_0, out_1, out_2
+):
+    nc = tc.nc
+    with ExitStack() as ctx:
+        keep = ctx.enter_context(tc.tile_pool(name="keep", bufs=1))
+        psum = ctx.enter_context(tc.psum_pool(name="psum", bufs=1))
+
+        def sb(name, shape, dtype, tag=None):
+            return keep.tile(shape, dtype, name=name, tag=tag or name, align_bytes=64)
+
+        def load_list(name, src):
+            tile = sb(name, list(src.shape), U16)
+            nc.sync.dma_start(tile[:], src)
+            return tile
+
+        def as_words(src):
+            return src[0].rearrange("p n t -> p (n t)").bitcast(I32)
+
+        k1_sc = sb("k1_sc", [P, TABLE], U8, tag="shared")
+        d_sc = sb("d_sc", [P, TABLE], U8)
+        x_sc = sb("x_sc", [P, TABLE], U8)
+        k1_plane = sb("k1_plane", [P, S], U8)
+        nc.vector.memset(k1_sc[:, 0 : TABLE // 2].bitcast(I32), 0)
+        nc.gpsimd.memset(k1_sc[:, TABLE // 2 : TABLE].bitcast(I32), 0)
+        for tile in (d_sc, x_sc, k1_plane):
+            nc.vector.memset(tile[:].bitcast(I32), 0)
+
+        gs_raw = sb("gs_raw", [P, PACK], F32)
+        nc.gpsimd.dma_start(gs_raw[:], gs.rearrange("(p t) o -> p (t o)", t=PACK))
+        k1_l = load_list("k1_l", k1)
+        ci_l = load_list("ci_l", ci)
+        offs_l = load_list("offs_l", offs)
+        n1_l = load_list("n1_l", n1)
+        n2_l = load_list("n2_l", n2)
+        n3_l = load_list("n3_l", n3)
+        d_rows = d_scales[0].bitcast(I32)
+        nc.sync.dma_start(k1_sc[0:P:8, :].bitcast(I32), d_rows)
+        d_w = sb("d_w", [P, TABLE], I32)
+        nc.sync.dma_start(d_w[:], as_words(d_words))
+        for r in range(4):
+            nc.sync.dma_start(d_sc[r:P:32, :].bitcast(I32), d_rows[r:16:4, :])
+        x_rows = x_scales[0].bitcast(I32)
+        for r in range(4):
+            queue = nc.sync if r < 2 else nc.gpsimd
+            queue.dma_start(x_sc[r:P:32, :].bitcast(I32), x_rows[r:16:4, :])
+
+        gs16 = sb("gs16", [P, PACK], F32)
+        nc.scalar.mul(gs16[:], gs_raw[:], 0.0625)
+
+        k1_b = sb("k1_b", [P, S], U8)
+        nc.vector.tensor_copy(k1_b[:], k1_sc[:].indirect(k1_l[:]))
+        x_w = sb("x_w", [P, TABLE], I32, tag="shared")
+        nc.sync.dma_start(x_w[:], as_words(x_words))
+        k1_bd = sb("k1_bd", [P, S], U8)
+        nc.vector.tensor_copy(
+            k1_bd[:].rearrange("p (t b i) -> p b t i", t=PACK, i=16),
+            k1_b[:].rearrange("p (b i t) -> p b t i", t=PACK, i=16),
+        )
+        for q in range(4):
+            nc.scalar.dma_start(
+                k1_plane[32 * q : 32 * q + 4, :].bitcast(I32),
+                k1_bd[32 * q : 32 * q + 32 : 8, :].bitcast(I32),
+            )
+        ci_b = sb("ci_b", [P, S], U8)
+        nc.vector.tensor_copy(ci_b[:].rearrange("p (t m) -> p m t", t=PACK), d_sc[:].indirect(ci_l[:]))
+        ci_w = sb("ci_w", [P, S], U32)
+        nc.vector.tensor_copy(ci_w[:].rearrange("p (t m) -> p m t", t=PACK), d_w[:].bitcast(U32).indirect(ci_l[:]))
+        x_b = sb("x_b", [P, S], U8)
+        nc.vector.tensor_copy(x_b[:], x_sc[:].indirect(offs_l[:]))
+        x_half = []
+        for u in range(2):
+            xh = sb("x_half%d" % u, [P, HALF], U32)
+            nc.vector.tensor_copy(xh[:], x_w[:].bitcast(U32).indirect(offs_l[:, 16 * u : 16 * (u + 1)]))
+            x_half.append(xh)
+        k1_w = sb("k1_w", [P, S], U32, tag="shared")
+        nc.vector.tensor_copy(k1_w[:], d_w[:].bitcast(U32).indirect(k1_l[:]))
+        k1_wd = sb("k1_wd", [P, S], U32)
+        dealt = k1_wd[:].rearrange("p (t b i) -> p b t i", t=PACK, i=4)
+        listed = k1_w[:].rearrange("p (b i t) -> p b t i", t=PACK, i=4)
+        nc.vector.tensor_copy(dealt[:, :, 0:1, :], listed[:, :, 0:1, :])
+
+        def product1(out, t, u, c0, n):
+            nc.tensor.matmul_mx(
+                out=out,
+                lhsT=ci_w[:, P * t : P * (t + 1)].bitcast(FP8X4),
+                lhsT_scale=ci_b[:, P * t : P * (t + 1)],
+                rhs=x_half[u][:, c0 : c0 + n].bitcast(FP8X4),
+                rhs_scale=x_b[:, HALF * u + c0 : HALF * u + c0 + n],
+                start=True,
+                stop=True,
+            )
+
+        z_flat = sb("z_flat", [P, PACK, HALF], BF16)
+        for t in range(PACK):
+            bank = psum.tile([P, S], F32, name="s_a%d" % t, tag="bank%d" % t)
+            product1(bank[:, 0:HALF], t, 0, 0, HALF)
+            nc.scalar.activation(z_flat[:, t, :], bank[:, 0:HALF], COPY, scale=gs16[:, t : t + 1])
+        z_in = [sb("z_in%d" % u, [P, HALF, PACK], BF16) for u in range(2)]
+        nc.scalar.copy(
+            z_in[0][:].rearrange("p (c i) t -> p c t i", i=4),
+            z_flat[:].rearrange("p t (c i) -> p c t i", i=4),
+        )
+        for v in range(2):
+            bank = psum.tile([P, PACK, QUARTER], F32, name="s_b%d" % v, tag="bank%d" % (4 + v))
+            for t in range(PACK):
+                product1(bank[:, t, :], t, 1, QUARTER * v, QUARTER)
+            nc.vector.tensor_tensor(
+                z_in[1][:, QUARTER * v : QUARTER * (v + 1), :],
+                bank[:].rearrange("p t n -> p n t"),
+                gs16[:].unsqueeze(1).to_broadcast([P, QUARTER, PACK]),
+                ALU.mult,
+            )
+        z_w = sb("z_w", [P, S], U32)
+        z_b = sb("z_b", [P, S], U8)
+        for u in (1, 0):
+            nc.vector.quantize_mx(
+                out=z_w[:, HALF * u : HALF * (u + 1)].bitcast(FP8X4),
+                scales=z_b[:, HALF * u : HALF * (u + 1)],
+                in_=z_in[u][:].rearrange("p c t -> p (c t)"),
+            )
+
+        nc.vector.tensor_copy(dealt[:, :, 1:PACK, :], listed[:, :, 1:PACK, :])
+
+        def product2(out, t, c0, n):
+            nc.tensor.matmul_mx(
+                out=out,
+                lhsT=k1_wd[:, P * t : P * (t + 1)].bitcast(FP8X4),
+                lhsT_scale=k1_plane[:, P * t : P * (t + 1)],
+                rhs=z_w[:, c0 : c0 + n].bitcast(FP8X4),
+                rhs_scale=z_b[:, c0 : c0 + n],
+                start=True,
+                stop=True,
+            )
+
+        h = [sb("h%d" % t, [P, S], F32) for t in range(PACK)]
+        pa = [sb("pa%d" % t, [P, HALF], F32) for t in range(PACK)]
+        pb = [sb("pb%d" % t, [P, HALF], F32) for t in range(PACK)]
+        ra = [sb("ra%d" % t, [P, HALF], F32) for t in range(PACK)]
+        rb = [sb("rb%d" % t, [P, HALF], F32) for t in range(PACK)]
+        dt_ = [sb("dt%d" % t, [P, S], F32) for t in range(PACK)]
+        far = [sb("far%d" % t, [P, S], F32) for t in range(PACK)]
+        y = sb("y", [P, PACK, S], F32)
+        out_rows = out_0.rearrange("(p t) c -> p t c", t=PACK)
+
+        def make_h(t):
+            if t == 0:
+                for u in (1, 0):
+                    bank = psum.tile([P, HALF], F32, name="h0_%d" % u, tag="bank%d" % (6 + u))
+                    product2(bank[:], 0, HALF * u, HALF)
+                    nc.scalar.mul(h[0][:, HALF * u : HALF * (u + 1)], bank[:], 0.0625)
+            else:
+                bank = psum.tile([P, S], F32, name="h_bank%d" % t, tag="bank%d" % t)
+                product2(bank[:], t, 0, S)
+                nc.scalar.mul(h[t][:], bank[:], 0.0625)
+            nc.scalar.activation(pa[t][:], h[t][:].indirect(n1_l[:]), COPY)
+            if t == 0:
+                nc.vector.tensor_copy(pb[t][:], h[t][:].indirect(n2_l[:]))
+            else:
+                nc.scalar.activation(pb[t][:], h[t][:].indirect(n2_l[:]), COPY)
+
+        def sort_pairs(t):
+            nc.vector.tensor_tensor(ra[t][:], pa[t][:], pb[t][:], ALU.max)
+            nc.vector.tensor_tensor(rb[t][:], pa[t][:], pb[t][:], ALU.min)
+            nc.vector.tensor_copy(dt_[t][:].indirect(n1_l[:]), ra[t][:])
+            nc.vector.tensor_copy(dt_[t][:].indirect(n2_l[:]), rb[t][:])
+
+        def fetch_far(t):
+            for u in range(2):
+                nc.scalar.activation(
+                    far[t][:, HALF * u : HALF * (u + 1)], dt_[t][:].indirect(n3_l[:, 16 * u : 16 * (u + 1)]), COPY
+                )
+
+        def subtract(t, c0, n):
+            nc.vector.tensor_tensor(y[:, t, c0 : c0 + n], dt_[t][:, c0 : c0 + n], far[t][:, c0 : c0 + n], ALU.subtract)
+            nc.sync.dma_start(out_rows[:, t, c0 : c0 + n], y[:, t, c0 : c0 + n])
+
+        y_in = [sb("y_in%d" % u, [P, HALF, PACK], BF16) for u in range(2)]
+
+        def pair_views(u, t0):
+            return (
+                y_in[u][:, :, t0 : t0 + 2],
+                y[:, t0 : t0 + 2, HALF * u : HALF * (u + 1)].rearrange("p t c -> p c t"),
+            )
+
+        make_h(0)
+        make_h(1)
+        sort_pairs(0)
+        make_h(2)
+        sort_pairs(1)
+        fetch_far(0)
+        make_h(3)
+        subtract(0, 0, S)
+        sort_pairs(2)
+        fetch_far(1)
+        subtract(1, 0, S)
+        for u in range(2):
+            nc.scalar.copy(*pair_views(u, 0))
+        fetch_far(2)
+        sort_pairs(3)
+        subtract(2, 0, S)
+        fetch_far(3)
+
+        y_w = sb("y_w", [P, S], U32)
+        y_b = sb("y_b", [P, S], U8)
+        words_out = as_words(out_1)
+        for u in range(2):
+            subtract(3, HALF * u, HALF)
+            nc.vector.tensor_copy(*pair_views(u, 2))
+            nc.vector.quantize_mx(
+                out=y_w[:, HALF * u : HALF * (u + 1)].bitcast(FP8X4),
+                scales=y_b[:, HALF * u : HALF * (u + 1)],
+                in_=y_in[u][:].rearrange("p c t -> p (c t)"),
+            )
+            nc.sync.dma_start(words_out[:, HALF * u : HALF * (u + 1)], y_w[:, HALF * u : HALF * (u + 1)].bitcast(I32))
+        scale_rows = out_2[0].bitcast(I32)
+        for q in range(4):
+            queue = nc.scalar if q % 2 else nc.sync
+            queue.dma_start(scale_rows[4 * q : 4 * q + 4, :], y_b[32 * q : 32 * q + 4, :].bitcast(I32))

@@ -41,63 +41,61 @@ def tile_picked_dwqiordd_none_po_kernel(
         def as_words(src):
             return src[0].rearrange("p n t -> p (n t)").bitcast(I32)
 
-        k1_sc = sb("k1_sc", [P, TABLE], U8, tag="shared")
         d_sc = sb("d_sc", [P, TABLE], U8)
         x_sc = sb("x_sc", [P, TABLE], U8)
+        for tile in (d_sc, x_sc):
+            nc.vector.memset(tile[:, 0 : TABLE // 2].bitcast(I32), 0)
+            nc.gpsimd.memset(tile[:, TABLE // 2 : TABLE].bitcast(I32), 0)
+        plane1 = sb("plane1", [P, 2 * S], U8)
         k1_plane = sb("k1_plane", [P, S], U8)
-        nc.vector.memset(k1_sc[:, 0 : TABLE // 2].bitcast(I32), 0)
-        nc.gpsimd.memset(k1_sc[:, TABLE // 2 : TABLE].bitcast(I32), 0)
-        for tile in (d_sc, x_sc, k1_plane):
+        for tile in (plane1, k1_plane):
             nc.vector.memset(tile[:].bitcast(I32), 0)
 
         gs_raw = sb("gs_raw", [P, PACK], F32)
         nc.gpsimd.dma_start(gs_raw[:], gs.rearrange("(p t) o -> p (t o)", t=PACK))
-        k1_l = load_list("k1_l", k1)
         ci_l = load_list("ci_l", ci)
+        k1_l = load_list("k1_l", k1)
         offs_l = load_list("offs_l", offs)
         n1_l = load_list("n1_l", n1)
         n2_l = load_list("n2_l", n2)
         n3_l = load_list("n3_l", n3)
-        d_rows = d_scales[0].bitcast(I32)
-        nc.sync.dma_start(k1_sc[0:P:8, :].bitcast(I32), d_rows)
+        nc.sync.dma_start(d_sc[0:P:8, :].bitcast(I32), d_scales[0].bitcast(I32))
         d_w = sb("d_w", [P, TABLE], I32)
         nc.sync.dma_start(d_w[:], as_words(d_words))
-        for r in range(4):
-            nc.sync.dma_start(d_sc[r:P:32, :].bitcast(I32), d_rows[r:16:4, :])
-        x_rows = x_scales[0].bitcast(I32)
-        for r in range(4):
-            queue = nc.sync if r < 2 else nc.gpsimd
-            queue.dma_start(x_sc[r:P:32, :].bitcast(I32), x_rows[r:16:4, :])
+        nc.sync.dma_start(x_sc[0:P:8, :].bitcast(I32), x_scales[0].bitcast(I32))
+        x_w = sb("x_w", [P, TABLE], I32)
+        nc.sync.dma_start(x_w[:], as_words(x_words))
 
         gs16 = sb("gs16", [P, PACK], F32)
         nc.scalar.mul(gs16[:], gs_raw[:], 0.0625)
 
+        def move_rows(plane, spread):
+            for q in range(4):
+                queue = nc.scalar if q % 2 else nc.sync
+                queue.dma_start(
+                    plane[32 * q : 32 * q + 4, :].bitcast(I32), spread[32 * q : 32 * q + 32 : 8, :].bitcast(I32)
+                )
+
+        picked1 = sb("picked1", [P, 2 * S], U8)
+        nc.vector.tensor_copy(picked1[:, 0:S].rearrange("p (t m) -> p m t", t=PACK), d_sc[:].indirect(ci_l[:]))
         k1_b = sb("k1_b", [P, S], U8)
-        nc.vector.tensor_copy(k1_b[:], k1_sc[:].indirect(k1_l[:]))
-        x_w = sb("x_w", [P, TABLE], I32, tag="shared")
-        nc.sync.dma_start(x_w[:], as_words(x_words))
-        k1_bd = sb("k1_bd", [P, S], U8)
+        nc.vector.tensor_copy(k1_b[:], d_sc[:].indirect(k1_l[:]))
+        nc.vector.tensor_copy(picked1[:, S : 2 * S], x_sc[:].indirect(offs_l[:]))
+        move_rows(plane1, picked1)
+        k1_bd = sb("k1_bd", [P, S], U8, tag="x_sc")
         nc.vector.tensor_copy(
             k1_bd[:].rearrange("p (t b i) -> p b t i", t=PACK, i=16),
             k1_b[:].rearrange("p (b i t) -> p b t i", t=PACK, i=16),
         )
-        for q in range(4):
-            nc.scalar.dma_start(
-                k1_plane[32 * q : 32 * q + 4, :].bitcast(I32),
-                k1_bd[32 * q : 32 * q + 32 : 8, :].bitcast(I32),
-            )
-        ci_b = sb("ci_b", [P, S], U8)
-        nc.vector.tensor_copy(ci_b[:].rearrange("p (t m) -> p m t", t=PACK), d_sc[:].indirect(ci_l[:]))
-        ci_w = sb("ci_w", [P, S], U32)
+        move_rows(k1_plane, k1_bd)
+        ci_w = sb("ci_w", [P, S], U32, tag="k1_b")
         nc.vector.tensor_copy(ci_w[:].rearrange("p (t m) -> p m t", t=PACK), d_w[:].bitcast(U32).indirect(ci_l[:]))
-        x_b = sb("x_b", [P, S], U8)
-        nc.vector.tensor_copy(x_b[:], x_sc[:].indirect(offs_l[:]))
         x_half = []
         for u in range(2):
             xh = sb("x_half%d" % u, [P, HALF], U32)
             nc.vector.tensor_copy(xh[:], x_w[:].bitcast(U32).indirect(offs_l[:, 16 * u : 16 * (u + 1)]))
             x_half.append(xh)
-        k1_w = sb("k1_w", [P, S], U32, tag="shared")
+        k1_w = sb("k1_w", [P, S], U32, tag="x_w")
         nc.vector.tensor_copy(k1_w[:], d_w[:].bitcast(U32).indirect(k1_l[:]))
         k1_wd = sb("k1_wd", [P, S], U32)
         dealt = k1_wd[:].rearrange("p (t b i) -> p b t i", t=PACK, i=4)
@@ -108,9 +106,9 @@ def tile_picked_dwqiordd_none_po_kernel(
             nc.tensor.matmul_mx(
                 out=out,
                 lhsT=ci_w[:, P * t : P * (t + 1)].bitcast(FP8X4),
-                lhsT_scale=ci_b[:, P * t : P * (t + 1)],
+                lhsT_scale=plane1[:, P * t : P * (t + 1)],
                 rhs=x_half[u][:, c0 : c0 + n].bitcast(FP8X4),
-                rhs_scale=x_b[:, HALF * u + c0 : HALF * u + c0 + n],
+                rhs_scale=plane1[:, S + HALF * u + c0 : S + HALF * u + c0 + n],
                 start=True,
                 stop=True,
             )
@@ -121,10 +119,14 @@ def tile_picked_dwqiordd_none_po_kernel(
             product1(bank[:, 0:HALF], t, 0, 0, HALF)
             nc.scalar.activation(z_flat[:, t, :], bank[:, 0:HALF], COPY, scale=gs16[:, t : t + 1])
         z_in = [sb("z_in%d" % u, [P, HALF, PACK], BF16) for u in range(2)]
-        nc.scalar.copy(
-            z_in[0][:].rearrange("p (c i) t -> p c t i", i=4),
-            z_flat[:].rearrange("p t (c i) -> p c t i", i=4),
-        )
+
+        def weave_views(c0):
+            return (
+                z_in[0][:, c0 : c0 + QUARTER, :].rearrange("p (c i) t -> p c t i", i=4),
+                z_flat[:, :, c0 : c0 + QUARTER].rearrange("p t (c i) -> p c t i", i=4),
+            )
+
+        nc.scalar.copy(*weave_views(0))
         for v in range(2):
             bank = psum.tile([P, PACK, QUARTER], F32, name="s_b%d" % v, tag="bank%d" % (4 + v))
             for t in range(PACK):
@@ -135,6 +137,7 @@ def tile_picked_dwqiordd_none_po_kernel(
                 gs16[:].unsqueeze(1).to_broadcast([P, QUARTER, PACK]),
                 ALU.mult,
             )
+        nc.vector.tensor_copy(*weave_views(QUARTER))
         z_w = sb("z_w", [P, S], U32)
         z_b = sb("z_b", [P, S], U8)
         for u in (1, 0):
@@ -157,14 +160,14 @@ def tile_picked_dwqiordd_none_po_kernel(
                 stop=True,
             )
 
-        h = [sb("h%d" % t, [P, S], F32) for t in range(PACK)]
-        pa = [sb("pa%d" % t, [P, HALF], F32) for t in range(PACK)]
-        pb = [sb("pb%d" % t, [P, HALF], F32) for t in range(PACK)]
-        ra = [sb("ra%d" % t, [P, HALF], F32) for t in range(PACK)]
-        rb = [sb("rb%d" % t, [P, HALF], F32) for t in range(PACK)]
+        h = [sb("h%d" % t, [P, S], F32, tag=("h_a", "h_a", "h_b", "h_c")[t]) for t in range(PACK)]
+        pa = sb("pa", [P, PACK, HALF], F32)
+        pb = sb("pb", [P, PACK, HALF], F32)
+        ra = sb("ra", [P, PACK, HALF], F32)
+        rb = sb("rb", [P, PACK, HALF], F32)
         dt_ = [sb("dt%d" % t, [P, S], F32) for t in range(PACK)]
-        far = [sb("far%d" % t, [P, S], F32) for t in range(PACK)]
-        y = sb("y", [P, PACK, S], F32)
+        far = [sb("far%d" % t, [P, S], F32, tag=("h_c", "pb", "pb", "dt1")[t]) for t in range(PACK)]
+        y = [sb("y%d" % a, [P, 2, S], F32, tag=("pa", "y1")[a]) for a in range(2)]
         out_rows = out_0.rearrange("(p t) c -> p t c", t=PACK)
 
         def make_h(t):
@@ -174,20 +177,22 @@ def tile_picked_dwqiordd_none_po_kernel(
                     product2(bank[:], 0, HALF * u, HALF)
                     nc.scalar.mul(h[0][:, HALF * u : HALF * (u + 1)], bank[:], 0.0625)
             else:
-                bank = psum.tile([P, S], F32, name="h_bank%d" % t, tag="bank%d" % t)
+                bank = psum.tile([P, S], F32, name="h_bank%d" % t, tag="bank%d" % (0, 1, 6, 1)[t])
                 product2(bank[:], t, 0, S)
                 nc.scalar.mul(h[t][:], bank[:], 0.0625)
-            nc.scalar.activation(pa[t][:], h[t][:].indirect(n1_l[:]), COPY)
+            nc.scalar.activation(pa[:, t, :], h[t][:].indirect(n1_l[:]), COPY)
             if t == 0:
-                nc.vector.tensor_copy(pb[t][:], h[t][:].indirect(n2_l[:]))
+                nc.vector.tensor_copy(pb[:, t, :], h[t][:].indirect(n2_l[:]))
             else:
-                nc.scalar.activation(pb[t][:], h[t][:].indirect(n2_l[:]), COPY)
+                nc.scalar.activation(pb[:, t, :], h[t][:].indirect(n2_l[:]), COPY)
 
-        def sort_pairs(t):
-            nc.vector.tensor_tensor(ra[t][:], pa[t][:], pb[t][:], ALU.max)
-            nc.vector.tensor_tensor(rb[t][:], pa[t][:], pb[t][:], ALU.min)
-            nc.vector.tensor_copy(dt_[t][:].indirect(n1_l[:]), ra[t][:])
-            nc.vector.tensor_copy(dt_[t][:].indirect(n2_l[:]), rb[t][:])
+        def sort_pairs(t0, t1):
+            nc.vector.tensor_tensor(ra[:, t0:t1, :], pa[:, t0:t1, :], pb[:, t0:t1, :], ALU.max)
+            nc.vector.tensor_tensor(rb[:, t0:t1, :], pa[:, t0:t1, :], pb[:, t0:t1, :], ALU.min)
+            for t in range(t0, t1):
+                nc.vector.tensor_copy(dt_[t][:].indirect(n1_l[:]), ra[:, t, :])
+            for t in range(t0, t1):
+                nc.vector.tensor_copy(dt_[t][:].indirect(n2_l[:]), rb[:, t, :])
 
         def fetch_far(t):
             for u in range(2):
@@ -195,41 +200,40 @@ def tile_picked_dwqiordd_none_po_kernel(
                     far[t][:, HALF * u : HALF * (u + 1)], dt_[t][:].indirect(n3_l[:, 16 * u : 16 * (u + 1)]), COPY
                 )
 
-        def subtract(t, c0, n):
-            nc.vector.tensor_tensor(y[:, t, c0 : c0 + n], dt_[t][:, c0 : c0 + n], far[t][:, c0 : c0 + n], ALU.subtract)
-            nc.sync.dma_start(out_rows[:, t, c0 : c0 + n], y[:, t, c0 : c0 + n])
+        def subtract(engine, t, c0, n):
+            engine.tensor_tensor(y[t // 2][:, t % 2, c0 : c0 + n], dt_[t][:, c0 : c0 + n], far[t][:, c0 : c0 + n], ALU.subtract)
+            nc.sync.dma_start(out_rows[:, t, c0 : c0 + n], y[t // 2][:, t % 2, c0 : c0 + n])
 
         y_in = [sb("y_in%d" % u, [P, HALF, PACK], BF16) for u in range(2)]
 
         def pair_views(u, t0):
             return (
                 y_in[u][:, :, t0 : t0 + 2],
-                y[:, t0 : t0 + 2, HALF * u : HALF * (u + 1)].rearrange("p t c -> p c t"),
+                y[t0 // 2][:, :, HALF * u : HALF * (u + 1)].rearrange("p t c -> p c t"),
             )
 
         make_h(0)
         make_h(1)
-        sort_pairs(0)
+        sort_pairs(0, 1)
         make_h(2)
-        sort_pairs(1)
-        fetch_far(0)
+        sort_pairs(1, 2)
         make_h(3)
-        subtract(0, 0, S)
-        sort_pairs(2)
+        fetch_far(0)
+        sort_pairs(2, 4)
         fetch_far(1)
-        subtract(1, 0, S)
+        subtract(nc.gpsimd, 0, 0, S)
+        subtract(nc.gpsimd, 1, 0, S)
         for u in range(2):
             nc.scalar.copy(*pair_views(u, 0))
         fetch_far(2)
-        sort_pairs(3)
-        subtract(2, 0, S)
         fetch_far(3)
+        subtract(nc.vector, 2, 0, S)
 
         y_w = sb("y_w", [P, S], U32)
         y_b = sb("y_b", [P, S], U8)
         words_out = as_words(out_1)
         for u in range(2):
-            subtract(3, HALF * u, HALF)
+            subtract(nc.vector, 3, HALF * u, HALF)
             nc.vector.tensor_copy(*pair_views(u, 2))
             nc.vector.quantize_mx(
                 out=y_w[:, HALF * u : HALF * (u + 1)].bitcast(FP8X4),

@@ -28,6 +28,7 @@ def tile_picked_dwqiordd_none_po_kernel(
     nc = tc.nc
     with ExitStack() as ctx:
         keep = ctx.enter_context(tc.tile_pool(name="keep", bufs=1))
+        overlay = ctx.enter_context(tc.tile_pool(name="overlay", bufs=1))
         psum = ctx.enter_context(tc.psum_pool(name="psum", bufs=1))
 
         def sb(name, shape, dtype, tag=None):
@@ -63,16 +64,15 @@ def tile_picked_dwqiordd_none_po_kernel(
         d_w = sb("d_w", [P, TABLE], I32)
         nc.sync.dma_start(d_w[:], as_words(d_words))
         nc.sync.dma_start(x_sc[0:P:8, :].bitcast(I32), x_scales[0].bitcast(I32))
-        x_w = sb("x_w", [P, TABLE], I32)
+        x_w = overlay.tile([P, TABLE], I32, name="x_w", align_bytes=64, offset=0)
         nc.sync.dma_start(x_w[:], as_words(x_words))
 
         gs16 = sb("gs16", [P, PACK], F32)
         nc.scalar.mul(gs16[:], gs_raw[:], 0.0625)
 
-        def move_rows(plane, spread):
+        def move_rows(plane, spread, queues):
             for q in range(4):
-                queue = nc.scalar if q % 2 else nc.sync
-                queue.dma_start(
+                queues[q % len(queues)].dma_start(
                     plane[32 * q : 32 * q + 4, :].bitcast(I32), spread[32 * q : 32 * q + 32 : 8, :].bitcast(I32)
                 )
 
@@ -81,26 +81,23 @@ def tile_picked_dwqiordd_none_po_kernel(
         k1_b = sb("k1_b", [P, S], U8)
         nc.vector.tensor_copy(k1_b[:], d_sc[:].indirect(k1_l[:]))
         nc.vector.tensor_copy(picked1[:, S : 2 * S], x_sc[:].indirect(offs_l[:]))
-        move_rows(plane1, picked1)
-        k1_bd = sb("k1_bd", [P, S], U8, tag="x_sc")
-        nc.vector.tensor_copy(
-            k1_bd[:].rearrange("p (t b i) -> p b t i", t=PACK, i=16),
-            k1_b[:].rearrange("p (b i t) -> p b t i", t=PACK, i=16),
-        )
-        move_rows(k1_plane, k1_bd)
-        ci_w = sb("ci_w", [P, S], U32, tag="k1_b")
+        move_rows(plane1, picked1, (nc.sync, nc.scalar))
+        ci_w = sb("ci_w", [P, S], U32, tag="x_sc")
         nc.vector.tensor_copy(ci_w[:].rearrange("p (t m) -> p m t", t=PACK), d_w[:].bitcast(U32).indirect(ci_l[:]))
         x_half = []
         for u in range(2):
             xh = sb("x_half%d" % u, [P, HALF], U32)
             nc.vector.tensor_copy(xh[:], x_w[:].bitcast(U32).indirect(offs_l[:, 16 * u : 16 * (u + 1)]))
             x_half.append(xh)
-        k1_w = sb("k1_w", [P, S], U32, tag="x_w")
+        k1_bd = overlay.tile([P, S], U8, name="k1_bd", align_bytes=64, offset=0)
+        nc.vector.tensor_copy(
+            k1_bd[:].rearrange("p (t b i) -> p b t i", t=PACK, i=16),
+            k1_b[:].rearrange("p (b i t) -> p b t i", t=PACK, i=16),
+        )
+        move_rows(k1_plane, k1_bd, (nc.sync,))
+        k1_w = overlay.tile([P, S], U32, name="k1_w", align_bytes=64, offset=S)
         nc.vector.tensor_copy(k1_w[:], d_w[:].bitcast(U32).indirect(k1_l[:]))
-        k1_wd = sb("k1_wd", [P, S], U32)
-        dealt = k1_wd[:].rearrange("p (t b i) -> p b t i", t=PACK, i=4)
         listed = k1_w[:].rearrange("p (b i t) -> p b t i", t=PACK, i=4)
-        nc.vector.tensor_copy(dealt[:, :, 0:1, :], listed[:, :, 0:1, :])
 
         def product1(out, t, u, c0, n):
             nc.tensor.matmul_mx(
@@ -127,6 +124,7 @@ def tile_picked_dwqiordd_none_po_kernel(
             )
 
         nc.scalar.copy(*weave_views(0))
+        nc.scalar.copy(*weave_views(QUARTER))
         for v in range(2):
             bank = psum.tile([P, PACK, QUARTER], F32, name="s_b%d" % v, tag="bank%d" % (4 + v))
             for t in range(PACK):
@@ -137,22 +135,27 @@ def tile_picked_dwqiordd_none_po_kernel(
                 gs16[:].unsqueeze(1).to_broadcast([P, QUARTER, PACK]),
                 ALU.mult,
             )
-        nc.vector.tensor_copy(*weave_views(QUARTER))
+            if v == 0:
+                k1_first = sb("k1_first", [P, P], U32, tag="x_half0")
+                nc.vector.tensor_copy(k1_first[:].rearrange("p (t b i) -> p b t i", t=1, i=4), listed[:, :, 0:1, :])
         z_w = sb("z_w", [P, S], U32)
         z_b = sb("z_b", [P, S], U8)
-        for u in (1, 0):
+        z_pieces = ((0, QUARTER), (HALF, HALF), (QUARTER, QUARTER))
+        for c0, n in z_pieces:
             nc.vector.quantize_mx(
-                out=z_w[:, HALF * u : HALF * (u + 1)].bitcast(FP8X4),
-                scales=z_b[:, HALF * u : HALF * (u + 1)],
-                in_=z_in[u][:].rearrange("p c t -> p (c t)"),
+                out=z_w[:, c0 : c0 + n].bitcast(FP8X4),
+                scales=z_b[:, c0 : c0 + n],
+                in_=z_in[c0 // HALF][:, c0 % HALF : c0 % HALF + n, :].rearrange("p c t -> p (c t)"),
             )
 
-        nc.vector.tensor_copy(dealt[:, :, 1:PACK, :], listed[:, :, 1:PACK, :])
+        k1_rest = sb("k1_rest", [P, (PACK - 1) * P], U32, tag="z_in0")
+        nc.vector.tensor_copy(k1_rest[:].rearrange("p (t b i) -> p b t i", t=PACK - 1, i=4), listed[:, :, 1:PACK, :])
 
         def product2(out, t, c0, n):
+            k1_cols = k1_first[:] if t == 0 else k1_rest[:, P * (t - 1) : P * t]
             nc.tensor.matmul_mx(
                 out=out,
-                lhsT=k1_wd[:, P * t : P * (t + 1)].bitcast(FP8X4),
+                lhsT=k1_cols.bitcast(FP8X4),
                 lhsT_scale=k1_plane[:, P * t : P * (t + 1)],
                 rhs=z_w[:, c0 : c0 + n].bitcast(FP8X4),
                 rhs_scale=z_b[:, c0 : c0 + n],
@@ -160,7 +163,7 @@ def tile_picked_dwqiordd_none_po_kernel(
                 stop=True,
             )
 
-        h = [sb("h%d" % t, [P, S], F32, tag=("h_a", "h_a", "h_b", "h_c")[t]) for t in range(PACK)]
+        h = [sb("h%d" % t, [P, S], F32, tag=("h_a", "h_a", "h_a", "h_c")[t]) for t in range(PACK)]
         pa = sb("pa", [P, PACK, HALF], F32)
         pb = sb("pb", [P, PACK, HALF], F32)
         ra = sb("ra", [P, PACK, HALF], F32)
@@ -172,12 +175,12 @@ def tile_picked_dwqiordd_none_po_kernel(
 
         def make_h(t):
             if t == 0:
-                for u in (1, 0):
-                    bank = psum.tile([P, HALF], F32, name="h0_%d" % u, tag="bank%d" % (6 + u))
-                    product2(bank[:], 0, HALF * u, HALF)
-                    nc.scalar.mul(h[0][:, HALF * u : HALF * (u + 1)], bank[:], 0.0625)
+                for (c0, n), b in zip(z_pieces, (0, 7, 6)):
+                    bank = psum.tile([P, n], F32, name="h0_%d" % c0, tag="bank%d" % b)
+                    product2(bank[:], 0, c0, n)
+                    nc.scalar.mul(h[0][:, c0 : c0 + n], bank[:], 0.0625)
             else:
-                bank = psum.tile([P, S], F32, name="h_bank%d" % t, tag="bank%d" % (0, 1, 6, 1)[t])
+                bank = psum.tile([P, S], F32, name="h_bank%d" % t, tag="bank%d" % (0, 1, 2, 2)[t])
                 product2(bank[:], t, 0, S)
                 nc.scalar.mul(h[t][:], bank[:], 0.0625)
             nc.scalar.activation(pa[:, t, :], h[t][:].indirect(n1_l[:]), COPY)
@@ -186,13 +189,17 @@ def tile_picked_dwqiordd_none_po_kernel(
             else:
                 nc.scalar.activation(pb[:, t, :], h[t][:].indirect(n2_l[:]), COPY)
 
-        def sort_pairs(t0, t1):
+        def larger(t0, t1):
             nc.vector.tensor_tensor(ra[:, t0:t1, :], pa[:, t0:t1, :], pb[:, t0:t1, :], ALU.max)
+
+        def smaller(t0, t1):
             nc.vector.tensor_tensor(rb[:, t0:t1, :], pa[:, t0:t1, :], pb[:, t0:t1, :], ALU.min)
-            for t in range(t0, t1):
-                nc.vector.tensor_copy(dt_[t][:].indirect(n1_l[:]), ra[:, t, :])
-            for t in range(t0, t1):
-                nc.vector.tensor_copy(dt_[t][:].indirect(n2_l[:]), rb[:, t, :])
+
+        def put_larger(t):
+            nc.vector.tensor_copy(dt_[t][:].indirect(n1_l[:]), ra[:, t, :])
+
+        def put_smaller(t):
+            nc.vector.tensor_copy(dt_[t][:].indirect(n2_l[:]), rb[:, t, :])
 
         def fetch_far(t):
             for u in range(2):
@@ -214,12 +221,22 @@ def tile_picked_dwqiordd_none_po_kernel(
 
         make_h(0)
         make_h(1)
-        sort_pairs(0, 1)
+        larger(0, 1)
+        put_larger(0)
         make_h(2)
-        sort_pairs(1, 2)
+        larger(1, 2)
+        smaller(0, 2)
+        put_larger(1)
+        put_smaller(0)
+        put_smaller(1)
         make_h(3)
         fetch_far(0)
-        sort_pairs(2, 4)
+        larger(2, 4)
+        smaller(2, 4)
+        put_larger(2)
+        put_larger(3)
+        put_smaller(2)
+        put_smaller(3)
         fetch_far(1)
         subtract(nc.gpsimd, 0, 0, S)
         subtract(nc.gpsimd, 1, 0, S)

from contextlib import ExitStack

import concourse.mybir as mybir

F32 = mybir.dt.float32
BF16 = mybir.dt.bfloat16
I32 = mybir.dt.int32
U32 = mybir.dt.uint32
U16 = mybir.dt.uint16
U8 = mybir.dt.uint8
FP8X4 = mybir.dt.float8_e4m3fn_x4
ALU = mybir.AluOpType
COPY = mybir.ActivationFunctionType.Copy

P = 128
PACK = 4
TABLE = 2048
S = 512
HALF = S // 2
QUARTER = S // 4

FLOPS = 2 * 2 * 512 * 512 * 512


def tile_picked_dwqiordd_none_po_kernel(
    tc, x_words, x_scales, d_words, d_scales, gs, offs, ci, k1, n1, n2, n3, out_0, out_1, out_2
):
    nc = tc.nc
    with ExitStack() as ctx:
        keep = ctx.enter_context(tc.tile_pool(name="keep", bufs=1))
        overlay = ctx.enter_context(tc.tile_pool(name="overlay", bufs=1))
        psum = ctx.enter_context(tc.psum_pool(name="psum", bufs=1))

        def sb(name, shape, dtype, tag=None):
            return keep.tile(shape, dtype, name=name, tag=tag or name, align_bytes=64)

        def load_list(name, src):
            tile = sb(name, list(src.shape), U16)
            nc.sync.dma_start(tile[:], src)
            return tile

        def as_words(src):
            return src[0].rearrange("p n t -> p (n t)").bitcast(I32)

        d_sc = sb("d_sc", [P, TABLE], U8)
        x_sc = sb("x_sc", [P, TABLE], U8)
        for tile in (d_sc, x_sc):
            nc.vector.memset(tile[:, 0 : TABLE // 2].bitcast(I32), 0)
            nc.gpsimd.memset(tile[:, TABLE // 2 : TABLE].bitcast(I32), 0)
        plane1 = sb("plane1", [P, 2 * S], U8)
        k1_plane = sb("k1_plane", [P, S], U8)
        for tile in (plane1, k1_plane):
            nc.vector.memset(tile[:].bitcast(I32), 0)

        gs_raw = sb("gs_raw", [P, PACK], F32)
        nc.gpsimd.dma_start(gs_raw[:], gs.rearrange("(p t) o -> p (t o)", t=PACK))
        ci_l = load_list("ci_l", ci)
        k1_l = load_list("k1_l", k1)
        offs_l = load_list("offs_l", offs)
        n1_l = load_list("n1_l", n1)
        n2_l = load_list("n2_l", n2)
        n3_l = load_list("n3_l", n3)
        nc.sync.dma_start(d_sc[0:P:8, :].bitcast(I32), d_scales[0].bitcast(I32))
        d_w = sb("d_w", [P, TABLE], I32)
        nc.sync.dma_start(d_w[:], as_words(d_words))
        nc.sync.dma_start(x_sc[0:P:8, :].bitcast(I32), x_scales[0].bitcast(I32))
        x_w = overlay.tile([P, TABLE], I32, name="x_w", align_bytes=64, offset=0)
        nc.sync.dma_start(x_w[:], as_words(x_words))

        gs16 = sb("gs16", [P, PACK], F32)
        nc.scalar.mul(gs16[:], gs_raw[:], 0.0625)

        def move_rows(plane, spread, queues):
            for q in range(4):
                queues[q % len(queues)].dma_start(
                    plane[32 * q : 32 * q + 4, :].bitcast(I32), spread[32 * q : 32 * q + 32 : 8, :].bitcast(I32)
                )

        picked1 = sb("picked1", [P, 2 * S], U8)
        nc.vector.tensor_copy(picked1[:, 0:S].rearrange("p (t m) -> p m t", t=PACK), d_sc[:].indirect(ci_l[:]))
        k1_b = sb("k1_b", [P, S], U8)
        nc.vector.tensor_copy(k1_b[:], d_sc[:].indirect(k1_l[:]))
        nc.vector.tensor_copy(picked1[:, S : 2 * S], x_sc[:].indirect(offs_l[:]))
        move_rows(plane1, picked1, (nc.sync, nc.scalar))
        ci_w = sb("ci_w", [P, S], U32, tag="x_sc")
        nc.vector.tensor_copy(ci_w[:].rearrange("p (t m) -> p m t", t=PACK), d_w[:].bitcast(U32).indirect(ci_l[:]))
        x_half = []
        for u in range(2):
            xh = sb("x_half%d" % u, [P, HALF], U32)
            nc.vector.tensor_copy(xh[:], x_w[:].bitcast(U32).indirect(offs_l[:, 16 * u : 16 * (u + 1)]))
            x_half.append(xh)
        k1_bd = overlay.tile([P, S], U8, name="k1_bd", align_bytes=64, offset=0)
        nc.vector.tensor_copy(
            k1_bd[:].rearrange("p (t b i) -> p b t i", t=PACK, i=16),
            k1_b[:].rearrange("p (b i t) -> p b t i", t=PACK, i=16),
        )
        move_rows(k1_plane, k1_bd, (nc.sync,))
        k1_w = overlay.tile([P, S], U32, name="k1_w", align_bytes=64, offset=S)
        nc.vector.tensor_copy(k1_w[:], d_w[:].bitcast(U32).indirect(k1_l[:]))
        listed = k1_w[:].rearrange("p (b i t) -> p b t i", t=PACK, i=4)

        def product1(out, t, u, c0, n):
            nc.tensor.matmul_mx(
                out=out,
                lhsT=ci_w[:, P * t : P * (t + 1)].bitcast(FP8X4),
                lhsT_scale=plane1[:, P * t : P * (t + 1)],
                rhs=x_half[u][:, c0 : c0 + n].bitcast(FP8X4),
                rhs_scale=plane1[:, S + HALF * u + c0 : S + HALF * u + c0 + n],
                start=True,
                stop=True,
            )

        z_flat = sb("z_flat", [P, PACK, HALF], BF16)
        for t in range(PACK):
            bank = psum.tile([P, S], F32, name="s_a%d" % t, tag="bank%d" % t)
            product1(bank[:, 0:HALF], t, 0, 0, HALF)
            nc.scalar.activation(z_flat[:, t, :], bank[:, 0:HALF], COPY, scale=gs16[:, t : t + 1])
        z_in = [sb("z_in%d" % u, [P, HALF, PACK], BF16) for u in range(2)]

        def weave_views(c0):
            return (
                z_in[0][:, c0 : c0 + QUARTER, :].rearrange("p (c i) t -> p c t i", i=4),
                z_flat[:, :, c0 : c0 + QUARTER].rearrange("p t (c i) -> p c t i", i=4),
            )

        nc.scalar.copy(*weave_views(0))
        nc.scalar.copy(*weave_views(QUARTER))
        for v in range(2):
            bank = psum.tile([P, PACK, QUARTER], F32, name="s_b%d" % v, tag="bank%d" % (4 + v))
            for t in range(PACK):
                product1(bank[:, t, :], t, 1, QUARTER * v, QUARTER)
            nc.vector.tensor_tensor(
                z_in[1][:, QUARTER * v : QUARTER * (v + 1), :],
                bank[:].rearrange("p t n -> p n t"),
                gs16[:].unsqueeze(1).to_broadcast([P, QUARTER, PACK]),
                ALU.mult,
            )
            if v == 0:
                k1_first = sb("k1_first", [P, P], U32, tag="x_half0")
                nc.vector.tensor_copy(k1_first[:].rearrange("p (t b i) -> p b t i", t=1, i=4), listed[:, :, 0:1, :])
        z_w = sb("z_w", [P, S], U32)
        z_b = sb("z_b", [P, S], U8)
        z_pieces = ((0, QUARTER), (HALF, HALF), (QUARTER, QUARTER))
        for c0, n in z_pieces:
            nc.vector.quantize_mx(
                out=z_w[:, c0 : c0 + n].bitcast(FP8X4),
                scales=z_b[:, c0 : c0 + n],
                in_=z_in[c0 // HALF][:, c0 % HALF : c0 % HALF + n, :].rearrange("p c t -> p (c t)"),
            )

        k1_rest = sb("k1_rest", [P, (PACK - 1) * P], U32, tag="z_in0")
        nc.vector.tensor_copy(k1_rest[:].rearrange("p (t b i) -> p b t i", t=PACK - 1, i=4), listed[:, :, 1:PACK, :])

        def product2(out, t, c0, n):
            k1_cols = k1_first[:] if t == 0 else k1_rest[:, P * (t - 1) : P * t]
            nc.tensor.matmul_mx(
                out=out,
                lhsT=k1_cols.bitcast(FP8X4),
                lhsT_scale=k1_plane[:, P * t : P * (t + 1)],
                rhs=z_w[:, c0 : c0 + n].bitcast(FP8X4),
                rhs_scale=z_b[:, c0 : c0 + n],
                start=True,
                stop=True,
            )

        h = [sb("h%d" % t, [P, S], F32, tag=("h_a", "h_a", "h_a", "h_c")[t]) for t in range(PACK)]
        pa = sb("pa", [P, PACK, HALF], F32)
        pb = sb("pb", [P, PACK, HALF], F32)
        ra = sb("ra", [P, PACK, HALF], F32)
        rb = sb("rb", [P, PACK, HALF], F32)
        dt_ = [sb("dt%d" % t, [P, S], F32) for t in range(PACK)]
        far = [sb("far%d" % t, [P, S], F32, tag=("h_c", "pb", "pb", "dt1")[t]) for t in range(PACK)]
        y = [sb("y%d" % a, [P, 2, S], F32, tag=("pa", "y1")[a]) for a in range(2)]
        out_rows = out_0.rearrange("(p t) c -> p t c", t=PACK)

        def make_h(t):
            if t == 0:
                for (c0, n), b in zip(z_pieces, (0, 7, 6)):
                    bank = psum.tile([P, n], F32, name="h0_%d" % c0, tag="bank%d" % b)
                    product2(bank[:], 0, c0, n)
                    nc.scalar.mul(h[0][:, c0 : c0 + n], bank[:], 0.0625)
            else:
                bank = psum.tile([P, S], F32, name="h_bank%d" % t, tag="bank%d" % (0, 1, 2, 2)[t])
                product2(bank[:], t, 0, S)
                nc.scalar.mul(h[t][:], bank[:], 0.0625)
            nc.scalar.activation(pa[:, t, :], h[t][:].indirect(n1_l[:]), COPY)
            if t == 0:
                nc.vector.tensor_copy(pb[:, t, :], h[t][:].indirect(n2_l[:]))
            else:
                nc.scalar.activation(pb[:, t, :], h[t][:].indirect(n2_l[:]), COPY)

        def larger(t0, t1):
            nc.vector.tensor_tensor(ra[:, t0:t1, :], pa[:, t0:t1, :], pb[:, t0:t1, :], ALU.max)

        def smaller(t0, t1):
            nc.vector.tensor_tensor(rb[:, t0:t1, :], pa[:, t0:t1, :], pb[:, t0:t1, :], ALU.min)

        def put_larger(t):
            nc.vector.tensor_copy(dt_[t][:].indirect(n1_l[:]), ra[:, t, :])

        def put_smaller(t):
            nc.vector.tensor_copy(dt_[t][:].indirect(n2_l[:]), rb[:, t, :])

        def fetch_far(t):
            for u in range(2):
                nc.scalar.activation(
                    far[t][:, HALF * u : HALF * (u + 1)], dt_[t][:].indirect(n3_l[:, 16 * u : 16 * (u + 1)]), COPY
                )

        def subtract(engine, t, c0, n):
            engine.tensor_tensor(y[t // 2][:, t % 2, c0 : c0 + n], dt_[t][:, c0 : c0 + n], far[t][:, c0 : c0 + n], ALU.subtract)
            nc.sync.dma_start(out_rows[:, t, c0 : c0 + n], y[t // 2][:, t % 2, c0 : c0 + n])

        y_in = [sb("y_in%d" % u, [P, HALF, PACK], BF16) for u in range(2)]

        def pair_views(u, t0):
            return (
                y_in[u][:, :, t0 : t0 + 2],
                y[t0 // 2][:, :, HALF * u : HALF * (u + 1)].rearrange("p t c -> p c t"),
            )

        make_h(0)
        make_h(1)
        larger(0, 1)
        put_larger(0)
        make_h(2)
        larger(1, 2)
        smaller(0, 2)
        put_larger(1)
        put_smaller(0)
        put_smaller(1)
        make_h(3)
        fetch_far(0)
        larger(2, 4)
        smaller(2, 4)
        put_larger(2)
        put_larger(3)
        put_smaller(2)
        put_smaller(3)
        fetch_far(1)
        subtract(nc.gpsimd, 0, 0, S)
        subtract(nc.gpsimd, 1, 0, S)
        for u in range(2):
            nc.scalar.copy(*pair_views(u, 0))
        fetch_far(2)
        fetch_far(3)
        subtract(nc.vector, 2, 0, S)

        y_w = sb("y_w", [P, S], U32)
        y_b = sb("y_b", [P, S], U8)
        words_out = as_words(out_1)
        for u in range(2):
            subtract(nc.vector, 3, HALF * u, HALF)
            nc.vector.tensor_copy(*pair_views(u, 2))
            nc.vector.quantize_mx(
                out=y_w[:, HALF * u : HALF * (u + 1)].bitcast(FP8X4),
                scales=y_b[:, HALF * u : HALF * (u + 1)],
                in_=y_in[u][:].rearrange("p c t -> p (c t)"),
            )
            nc.sync.dma_start(words_out[:, HALF * u : HALF * (u + 1)], y_w[:, HALF * u : HALF * (u + 1)].bitcast(I32))
        scale_rows = out_2[0].bitcast(I32)
        for q in range(4):
            queue = nc.scalar if q % 2 else nc.sync
            queue.dma_start(scale_rows[4 * q : 4 * q + 4, :], y_b[32 * q : 32 * q + 4, :].bitcast(I32))
